import numpy as np
import ml_dtypes


def mxq(x, axis, fmt="e4m3"):
    dtype, down = {"e4m3": (ml_dtypes.float8_e4m3fn, 7), "e5m2": (ml_dtypes.float8_e5m2, 14)}[fmt]
    v = np.moveaxis(np.asarray(x, np.float32).astype(ml_dtypes.bfloat16).astype(np.float64), axis, -1)
    blocks = v.reshape(v.shape[:-1] + (-1, 32))
    amax = np.abs(blocks).max(-1, keepdims=True)
    byte = np.maximum(np.where(amax > 0, np.frexp(amax)[1] - 1 + 127, 0) - down, 1)
    scale = np.exp2(byte - 127.0)
    codes = (blocks / scale).astype(np.float32).astype(dtype).astype(np.float64)
    return np.moveaxis((codes * scale).reshape(v.shape), -1, axis)


WIDE = False


def mx_kscale(k):
    if not WIDE:
        return np.ones(k)
    levels = np.array([10, -10, 5, -5, 0])
    if k % 512:
        return np.exp2(np.random.permutation(np.resize(levels, k // 32))).repeat(32)
    a = np.empty((k // 512, 16))
    for p in range(k // 512):
        a[p, :8] = np.random.permutation(np.resize(levels, 8))
        for g in range(8):
            far = levels[np.abs(levels - a[p, g]) >= 10]
            a[p, g + 8] = far[np.random.randint(len(far))]
    return np.exp2(a.ravel()).repeat(32)


def f64(x):
    return np.asarray(x).astype(np.float64)


def striped8(idx):
    return np.asarray(idx).reshape(8, -1, 16).transpose(0, 2, 1).reshape(128, -1).astype(np.uint16)


def unstriped8(offs):
    return offs.reshape(8, 16, -1).transpose(0, 2, 1).reshape(8, -1).astype(np.int64)


def pick8(x, idx, run):
    r = np.arange(len(x))
    return x[r[:, None], idx[r % (8 * run) // run]]


E2M1 = np.array([0.0, 0.5, 1.0, 1.5, 2.0, 3.0, 4.0, 6.0, -0.0, -0.5, -1.0, -1.5, -2.0, -3.0, -4.0, -6.0])


def pack_weight(w, fmt):
    k, n = w.shape
    w = f64(np.asarray(w, np.float32).astype(ml_dtypes.bfloat16)).reshape(k // 32, 32, n)
    amax = np.abs(w).max(1)
    if fmt == "e4m3":
        byte = np.frexp(amax)[1] - 1 + 127 - 7
    else:
        mant, ex = np.frexp(amax / 6.0)
        byte = np.where(mant > 0.5, ex, ex - 1) + 127
    byte = np.clip(np.where(amax > 0, byte, 1), 1, 254)
    scaled = (w * np.exp2(127.0 - byte)[:, None, :]).reshape(k, n).astype(np.float32)
    by_word = np.ascontiguousarray(scaled.reshape(k // 512, 128, 4, n).transpose(0, 1, 3, 2))
    if fmt == "e4m3":
        words = by_word.astype(ml_dtypes.float8_e4m3fn).view(np.uint8)
    else:
        c = by_word.astype(ml_dtypes.float4_e2m1fn).view(np.uint8) & 0xF
        words = (c[..., 0::2] | (c[..., 1::2] << 4)).reshape(k // 512, 128, 2 * n)
    return np.ascontiguousarray(words), np.ascontiguousarray(byte.astype(np.uint8).reshape(k // 512, 16, n))


def unpack_weight(words, scales, fmt):
    g, _, n = scales.shape
    words = np.ascontiguousarray(words).reshape(g, 128, n, -1)
    if fmt == "e4m3":
        vals = words.view(ml_dtypes.float8_e4m3fn).astype(np.float64)
    else:
        nib = np.empty((g, 128, n, 4), np.uint8)
        nib[..., 0::2] = words & 0xF
        nib[..., 1::2] = words >> 4
        vals = E2M1[nib]
    vals = vals * np.repeat(np.exp2(scales.astype(np.float64) - 127.0), 8, axis=1)[..., None]
    return vals.transpose(0, 1, 3, 2).reshape(g * 512, n)


def sigmoid(v):
    return 1.0 / (1.0 + np.exp(-v))


D, K, T, U, I, Q = 512, 512, 1024, 1024, 512, 128


def setup_inputs():
    n = np.random.standard_normal
    idx = np.stack([np.random.permutation(T)[:I] for _ in range(8)])
    idx2 = np.stack([np.random.permutation(U)[:I] for _ in range(8)])
    idx3 = np.stack([np.random.permutation(T)[:I] for _ in range(8)])
    fd = mx_kscale(D)
    fk = mx_kscale(K)
    wqp = pack_weight(n((D, K)) * 1.0 / np.sqrt(D) * fd[:, None] * fk, "e4m3")
    keysp = pack_weight(n((K, T)) * 1.0 / np.sqrt(K) / fk[:, None], "e2m1")
    notesp = pack_weight(n((D, U)) * 1.0 / np.sqrt(D) * fd[:, None], "e4m3")
    return {
        "states": (n((D, Q)) * 0.95 / fd[:, None]).astype(np.float32),
        "wq_words": wqp[0],
        "wq_scales": wqp[1],
        "keys_words": keysp[0],
        "keys_scales": keysp[1],
        "notes_words": notesp[0],
        "notes_scales": notesp[1],
        "thr": (np.random.uniform(-0.6, 0.6, (Q, 1))).astype(np.float32),
        "slope": (np.random.uniform(1.0, 3.0, (Q, 1))).astype(np.float32),
        "old": (1.0 * n((Q, T))).astype(np.float32),
        "offs": striped8(idx),
        "offs2": striped8(idx2),
        "offs3": striped8(idx3),
    }


def reference(states, wq_words, wq_scales, keys_words, keys_scales, notes_words, notes_scales, thr, slope, old, offs, offs2, offs3):
    idx = unstriped8(offs)
    idx2 = unstriped8(offs2)
    idx3 = unstriped8(offs3)
    wqu = unpack_weight(wq_words, wq_scales, "e4m3")
    keysu = unpack_weight(keys_words, keys_scales, "e2m1")
    notesu = unpack_weight(notes_words, notes_scales, "e4m3")
    statesq = mxq(f64(states), 0, "e4m3")
    qv = wqu.T @ statesq
    qvq = mxq(qv, 0, "e4m3")
    a = qvq.T @ keysu
    b = statesq.T @ notesu
    e2 = sigmoid(pick8(b, idx2, 16) * f64(slope) + f64(thr))
    w = pick8(a, idx, 16) * e2
    f1 = np.zeros((Q, T))
    f1[np.arange(Q)[:, None], idx[np.arange(Q) % 128 // 16]] = w
    tt = f64(old) + f1
    y = pick8(tt, idx3, 16)
    return y

@@ -1,0 +1,139 @@
+from contextlib import ExitStack
+
+import concourse.mybir as mybir
+
+D, K, T, U, I, Q = 512, 512, 1024, 1024, 512, 128
+FLOPS = 2 * D * K * Q + 2 * K * Q * T + 2 * D * Q * U
+
+F32 = mybir.dt.float32
+BF16 = mybir.dt.bfloat16
+I32 = mybir.dt.int32
+U32 = mybir.dt.uint32
+U16 = mybir.dt.uint16
+U8 = mybir.dt.uint8
+FP8X4 = mybir.dt.float8_e4m3fn_x4
+FP4X4 = mybir.dt.float4_e2m1fn_x4
+ACT = mybir.ActivationFunctionType
+ALU = mybir.AluOpType
+
+P = 128
+PACK = 4
+HALF = I // 2
+LCOLS = HALF // 16
+
+
+def tile_attend_gateway_madeside_kernel(tc, states, wq_words, wq_scales, keys_words, keys_scales,
+                                         notes_words, notes_scales, thr, slope, old, offs, offs2, offs3, out):
+    nc = tc.nc
+    with ExitStack() as ctx:
+        sb = ctx.enter_context(tc.tile_pool(name="sb", bufs=1))
+        ps = ctx.enter_context(tc.psum_pool(name="ps", bufs=1))
+
+        wq_plane_raw = sb.tile([P, K], U8, align_bytes=64)
+        notes_plane = sb.tile([P, U], U8, align_bytes=64)
+        keys_plane = sb.tile([P, T], U8, align_bytes=64)
+        f1 = sb.tile([P, T], F32)
+        nc.vector.memset(wq_plane_raw[:].bitcast(I32), 0)
+        nc.vector.memset(keys_plane[:].bitcast(I32), 0)
+        nc.vector.memset(notes_plane[:].bitcast(I32), 0)
+        nc.vector.memset(f1[:], 0.0)
+
+        def load_plane(queues, plane, scales):
+            for quad in range(4):
+                queues[quad].dma_start(
+                    out=plane[32 * quad : 32 * quad + 4, :].bitcast(I32),
+                    in_=scales[0, 4 * quad : 4 * quad + 4, :].bitcast(I32),
+                )
+
+        states_raw = sb.tile([P, PACK, Q], F32)
+        nc.sync.dma_start(out=states_raw[:], in_=states.rearrange("(p j) q -> p j q", j=PACK))
+        wq_raw = sb.tile([P, K], U32)
+        nc.sync.dma_start(out=wq_raw[:].bitcast(I32), in_=wq_words[0].rearrange("p n t -> p (n t)").bitcast(I32))
+        load_plane([nc.scalar] * 4, wq_plane_raw, wq_scales)
+        notes_codes = sb.tile([P, U], U32, align_bytes=64)
+        nc.gpsimd.dma_start(out=notes_codes[:].bitcast(I32), in_=notes_words[0].rearrange("p n t -> p (n t)").bitcast(I32))
+        keys_codes = sb.tile([P, 2 * T], U8, align_bytes=64)
+        nc.gpsimd.dma_start(out=keys_codes[:].bitcast(I32), in_=keys_words[0].bitcast(I32))
+        load_plane([nc.sync] * 4, keys_plane, keys_scales)
+        load_plane([nc.scalar] * 4, notes_plane, notes_scales)
+        list2 = sb.tile([P, I // 16], U16)
+        nc.sync.dma_start(list2[:], offs2)
+        list1 = sb.tile([P, I // 16], U16)
+        nc.sync.dma_start(list1[:], offs)
+        slope_col = sb.tile([P, 1], F32)
+        nc.gpsimd.dma_start(out=slope_col[:], in_=slope)
+        thr_col = sb.tile([P, 1], F32)
+        nc.gpsimd.dma_start(out=thr_col[:], in_=thr)
+        list3 = sb.tile([P, I // 16], U16)
+        nc.sync.dma_start(list3[:], offs3)
+        old_sb = sb.tile([P, T], F32)
+        nc.sync.dma_start(out=old_sb[:], in_=old)
+
+        wq_plane = sb.tile([P, PACK, P], U8, align_bytes=64)
+        nc.vector.tensor_copy(out=wq_plane[:].rearrange("p t m -> p m t"),
+                              in_=wq_plane_raw[:].rearrange("p (m t) -> p m t", t=PACK))
+
+        states_bf = sb.tile([P, Q, PACK], BF16, align_bytes=64)
+        nc.vector.tensor_copy(out=states_bf[:], in_=states_raw[:].rearrange("p j q -> p q j"))
+        states_codes = sb.tile([P, Q], U32, align_bytes=64)
+        states_plane = sb.tile([P, Q], U8, align_bytes=64)
+        nc.vector.quantize_mx(out=states_codes[:].bitcast(FP8X4), scales=states_plane[:],
+                              in_=states_bf[:].rearrange("p q j -> p (q j)"))
+
+        wq_by_place = wq_raw[:].rearrange("p (m t) -> p m t", t=PACK)
+        wq_lo = sb.tile([P, 2, P], U32, align_bytes=64)
+        nc.scalar.copy(out=wq_lo[:].rearrange("p t m -> p m t"), in_=wq_by_place[:, :, 0:2])
+        wq_hi = sb.tile([P, 2, P], U32, align_bytes=64)
+        nc.vector.tensor_copy(out=wq_hi[:].bitcast(I32).rearrange("p t m -> p m t"),
+                              in_=wq_raw[:].bitcast(I32).rearrange("p (m t) -> p m t", t=PACK)[:, :, 2:4])
+
+        qv_ps = ps.tile([P, PACK, Q], F32)
+        for t in range(PACK):
+            wq_pair = wq_lo if t < 2 else wq_hi
+            nc.tensor.matmul_mx(out=qv_ps[:, t, :], lhsT=wq_pair[:, t % 2, :].bitcast(FP8X4), lhsT_scale=wq_plane[:, t, :],
+                                rhs=states_codes[:].bitcast(FP8X4), rhs_scale=states_plane[:], start=True, stop=True)
+        qv_bf = sb.tile([P, Q, PACK], BF16, align_bytes=64)
+        nc.scalar.copy(out=qv_bf[:], in_=qv_ps[:].rearrange("p t q -> p q t"))
+        qv_codes = sb.tile([P, Q], U32, align_bytes=64)
+        qv_plane = sb.tile([P, Q], U8, align_bytes=64)
+        nc.vector.quantize_mx(out=qv_codes[:].bitcast(FP8X4), scales=qv_plane[:],
+                              in_=qv_bf[:].rearrange("p q j -> p (q j)"))
+
+        b_sb = sb.tile([P, U], F32)
+        for h in range(2):
+            cols = slice(512 * h, 512 * (h + 1))
+            b_ps = ps.tile([P, 512], F32, name="b_ps%d" % h)
+            nc.tensor.matmul_mx(out=b_ps[:], lhsT=states_codes[:].bitcast(FP8X4), lhsT_scale=states_plane[:],
+                                rhs=notes_codes[:, cols].bitcast(FP8X4), rhs_scale=notes_plane[:, cols], start=True, stop=True)
+            if h == 0:
+                nc.scalar.copy(out=b_sb[:, cols], in_=b_ps[:])
+            else:
+                nc.vector.tensor_copy(out=b_sb[:, cols], in_=b_ps[:])
+
+        a_sb = sb.tile([P, T], F32)
+        for c in range(4):
+            cols = slice(256 * c, 256 * (c + 1))
+            a_ps = ps.tile([P, 256], F32, name="a_ps%d" % c)
+            nc.tensor.matmul_mx(out=a_ps[:], lhsT=qv_codes[:].bitcast(FP8X4), lhsT_scale=qv_plane[:],
+                                rhs=keys_codes[:, 512 * c : 512 * (c + 1)].bitcast(FP4X4), rhs_scale=keys_plane[:, cols],
+                                start=True, stop=True)
+            nc.vector.tensor_copy(out=a_sb[:, cols], in_=a_ps[:])
+
+        for h in range(2):
+            lc = slice(LCOLS * h, LCOLS * (h + 1))
+            e2 = sb.tile([P, HALF], F32, name="e2_%d" % h)
+            nc.scalar.activation(out=e2[:], in_=b_sb[:].indirect(list2[:, lc]), func=ACT.Sigmoid,
+                                 bias=thr_col[:], scale=slope_col[:])
+            picked = sb.tile([P, HALF], F32, name="picked_%d" % h)
+            nc.scalar.activation(out=picked[:], in_=a_sb[:].indirect(list1[:, lc]), func=ACT.Copy)
+            nc.vector.tensor_tensor(out=f1[:].indirect(list1[:, lc]), in0=picked[:], in1=e2[:], op=ALU.mult)
+
+        tt = sb.tile([P, T], F32)
+        nc.vector.tensor_tensor(out=tt[:], in0=f1[:], in1=old_sb[:], op=ALU.add)
+
+        y0 = sb.tile([P, HALF], F32)
+        nc.scalar.activation(out=y0[:], in_=tt[:].indirect(list3[:, 0:LCOLS]), func=ACT.Copy)
+        nc.scalar.dma_start(out=out[:, 0:HALF], in_=y0[:])
+        y1 = sb.tile([P, HALF], F32)
+        nc.vector.tensor_copy(out=y1[:], in_=tt[:].indirect(list3[:, LCOLS : 2 * LCOLS]))
+        nc.sync.dma_start(out=out[:, HALF:I], in_=y1[:])

@@ -34,44 +34,55 @@ def tile_attend_gateway_madeside_kernel(tc, states, wq_words, wq_scales, keys_wo
         keys_plane = sb.tile([P, T], U8, align_bytes=64)
         f1 = sb.tile([P, T], F32)
         nc.vector.memset(wq_plane_raw[:].bitcast(I32), 0)
-        nc.vector.memset(keys_plane[:].bitcast(I32), 0)
         nc.vector.memset(notes_plane[:].bitcast(I32), 0)
+        nc.vector.memset(keys_plane[:].bitcast(I32), 0)
+        warm_in = sb.tile([P, 1], F32)
+        nc.vector.memset(warm_in[:], 0.0)
         nc.vector.memset(f1[:], 0.0)
 
-        def load_plane(queues, plane, scales):
-            for quad in range(4):
-                queues[quad].dma_start(
-                    out=plane[32 * quad : 32 * quad + 4, :].bitcast(I32),
-                    in_=scales[0, 4 * quad : 4 * quad + 4, :].bitcast(I32),
-                )
+        def load_rows(queue, plane, scales, quad):
+            queue.dma_start(
+                out=plane[32 * quad : 32 * quad + 4, :].bitcast(I32),
+                in_=scales[0, 4 * quad : 4 * quad + 4, :].bitcast(I32),
+            )
 
         states_raw = sb.tile([P, PACK, Q], F32)
-        nc.sync.dma_start(out=states_raw[:], in_=states.rearrange("(p j) q -> p j q", j=PACK))
         wq_raw = sb.tile([P, K], U32)
-        nc.sync.dma_start(out=wq_raw[:].bitcast(I32), in_=wq_words[0].rearrange("p n t -> p (n t)").bitcast(I32))
-        load_plane([nc.scalar] * 4, wq_plane_raw, wq_scales)
         notes_codes = sb.tile([P, U], U32, align_bytes=64)
-        nc.gpsimd.dma_start(out=notes_codes[:].bitcast(I32), in_=notes_words[0].rearrange("p n t -> p (n t)").bitcast(I32))
         keys_codes = sb.tile([P, 2 * T], U8, align_bytes=64)
-        nc.gpsimd.dma_start(out=keys_codes[:].bitcast(I32), in_=keys_words[0].bitcast(I32))
-        load_plane([nc.sync] * 4, keys_plane, keys_scales)
-        load_plane([nc.scalar] * 4, notes_plane, notes_scales)
-        list2 = sb.tile([P, I // 16], U16)
-        nc.sync.dma_start(list2[:], offs2)
         list1 = sb.tile([P, I // 16], U16)
-        nc.sync.dma_start(list1[:], offs)
-        slope_col = sb.tile([P, 1], F32)
-        nc.gpsimd.dma_start(out=slope_col[:], in_=slope)
-        thr_col = sb.tile([P, 1], F32)
-        nc.gpsimd.dma_start(out=thr_col[:], in_=thr)
+        list2 = sb.tile([P, I // 16], U16)
         list3 = sb.tile([P, I // 16], U16)
-        nc.sync.dma_start(list3[:], offs3)
+        slope_col = sb.tile([P, 1], F32)
+        thr_col = sb.tile([P, 1], F32)
         old_sb = sb.tile([P, T], F32)
+
+        nc.sync.dma_start(out=states_raw[:], in_=states.rearrange("(p j) q -> p j q", j=PACK))
+        for quad in (0, 1):
+            load_rows(nc.sync, wq_plane_raw, wq_scales, quad)
+        nc.sync.dma_start(out=wq_raw[:].bitcast(I32), in_=wq_words[0].rearrange("p n t -> p (n t)").bitcast(I32))
+        load_rows(nc.sync, notes_plane, notes_scales, 0)
+        nc.sync.dma_start(out=notes_codes[:].bitcast(I32), in_=notes_words[0].rearrange("p n t -> p (n t)").bitcast(I32))
+        for quad in (1, 2):
+            load_rows(nc.sync, notes_plane, notes_scales, quad)
+        nc.sync.dma_start(out=keys_codes[:].bitcast(I32), in_=keys_words[0].bitcast(I32))
+        for quad in range(3):
+            load_rows(nc.sync, keys_plane, keys_scales, quad)
+        nc.sync.dma_start(list2[:], offs2)
+        nc.sync.dma_start(out=slope_col[:], in_=slope)
+        nc.sync.dma_start(out=thr_col[:], in_=thr)
+        nc.sync.dma_start(list1[:], offs)
+        nc.sync.dma_start(list3[:], offs3)
         nc.sync.dma_start(out=old_sb[:], in_=old)
 
-        wq_plane = sb.tile([P, PACK, P], U8, align_bytes=64)
-        nc.vector.tensor_copy(out=wq_plane[:].rearrange("p t m -> p m t"),
-                              in_=wq_plane_raw[:].rearrange("p (m t) -> p m t", t=PACK))
+        for quad in (2, 3):
+            load_rows(nc.scalar, wq_plane_raw, wq_scales, quad)
+
+        load_rows(nc.gpsimd, notes_plane, notes_scales, 3)
+        load_rows(nc.gpsimd, keys_plane, keys_scales, 3)
+
+        warm_out = sb.tile([P, 1], F32)
+        nc.scalar.activation(out=warm_out[:], in_=warm_in[:], func=ACT.Sigmoid)
 
         states_bf = sb.tile([P, Q, PACK], BF16, align_bytes=64)
         nc.vector.tensor_copy(out=states_bf[:], in_=states_raw[:].rearrange("p j q -> p q j"))
@@ -80,17 +91,22 @@ def tile_attend_gateway_madeside_kernel(tc, states, wq_words, wq_scales, keys_wo
         nc.vector.quantize_mx(out=states_codes[:].bitcast(FP8X4), scales=states_plane[:],
                               in_=states_bf[:].rearrange("p q j -> p (q j)"))
 
-        wq_by_place = wq_raw[:].rearrange("p (m t) -> p m t", t=PACK)
-        wq_lo = sb.tile([P, 2, P], U32, align_bytes=64)
-        nc.scalar.copy(out=wq_lo[:].rearrange("p t m -> p m t"), in_=wq_by_place[:, :, 0:2])
-        wq_hi = sb.tile([P, 2, P], U32, align_bytes=64)
-        nc.vector.tensor_copy(out=wq_hi[:].bitcast(I32).rearrange("p t m -> p m t"),
-                              in_=wq_raw[:].bitcast(I32).rearrange("p (m t) -> p m t", t=PACK)[:, :, 2:4])
+        words_by_place = wq_raw[:].rearrange("p (m t) -> p m t", t=PACK)
+        bytes_by_place = wq_plane_raw[:].rearrange("p (m t) -> p m t", t=PACK)
+        wq_codes = []
+        wq_planes = []
+        for pair in range(2):
+            places = slice(2 * pair, 2 * pair + 2)
+            codes = sb.tile([P, 2, P], U32, align_bytes=64, name="wq_codes%d" % pair)
+            nc.scalar.copy(out=codes[:].rearrange("p t m -> p m t"), in_=words_by_place[:, :, places])
+            plane = sb.tile([P, 2, P], U8, align_bytes=64, name="wq_plane%d" % pair)
+            nc.vector.tensor_copy(out=plane[:].rearrange("p t m -> p m t"), in_=bytes_by_place[:, :, places])
+            wq_codes.append(codes)
+            wq_planes.append(plane)
 
         qv_ps = ps.tile([P, PACK, Q], F32)
         for t in range(PACK):
-            wq_pair = wq_lo if t < 2 else wq_hi
-            nc.tensor.matmul_mx(out=qv_ps[:, t, :], lhsT=wq_pair[:, t % 2, :].bitcast(FP8X4), lhsT_scale=wq_plane[:, t, :],
+            nc.tensor.matmul_mx(out=qv_ps[:, t, :], lhsT=wq_codes[t // 2][:, t % 2, :].bitcast(FP8X4), lhsT_scale=wq_planes[t // 2][:, t % 2, :],
                                 rhs=states_codes[:].bitcast(FP8X4), rhs_scale=states_plane[:], start=True, stop=True)
         qv_bf = sb.tile([P, Q, PACK], BF16, align_bytes=64)
         nc.scalar.copy(out=qv_bf[:], in_=qv_ps[:].rearrange("p t q -> p q t"))
@@ -100,12 +116,12 @@ def tile_attend_gateway_madeside_kernel(tc, states, wq_words, wq_scales, keys_wo
                               in_=qv_bf[:].rearrange("p q j -> p (q j)"))
 
         b_sb = sb.tile([P, U], F32)
-        for h in range(2):
-            cols = slice(512 * h, 512 * (h + 1))
-            b_ps = ps.tile([P, 512], F32, name="b_ps%d" % h)
+        for first, last in ((0, 512), (512, 768), (768, 1024)):
+            cols = slice(first, last)
+            b_ps = ps.tile([P, last - first], F32, name="b_ps%d" % first)
             nc.tensor.matmul_mx(out=b_ps[:], lhsT=states_codes[:].bitcast(FP8X4), lhsT_scale=states_plane[:],
                                 rhs=notes_codes[:, cols].bitcast(FP8X4), rhs_scale=notes_plane[:, cols], start=True, stop=True)
-            if h == 0:
+            if first == 0:
                 nc.scalar.copy(out=b_sb[:, cols], in_=b_ps[:])
             else:
                 nc.vector.tensor_copy(out=b_sb[:, cols], in_=b_ps[:])

@@ -20,6 +20,7 @@ P = 128
 PACK = 4
 HALF = I // 2
 LCOLS = HALF // 16
+HEAD = 128
 
 
 def tile_attend_gateway_madeside_kernel(tc, states, wq_words, wq_scales, keys_words, keys_scales,
@@ -29,16 +30,14 @@ def tile_attend_gateway_madeside_kernel(tc, states, wq_words, wq_scales, keys_wo
         sb = ctx.enter_context(tc.tile_pool(name="sb", bufs=1))
         ps = ctx.enter_context(tc.psum_pool(name="ps", bufs=1))
 
-        wq_plane_raw = sb.tile([P, K], U8, align_bytes=64)
+        wq_plane_raw = sb.tile([P, K], U8, align_bytes=64, tag="wq_plane_then_f1")
         notes_plane = sb.tile([P, U], U8, align_bytes=64)
         keys_plane = sb.tile([P, T], U8, align_bytes=64)
-        f1 = sb.tile([P, T], F32)
         nc.vector.memset(wq_plane_raw[:].bitcast(I32), 0)
         nc.vector.memset(notes_plane[:].bitcast(I32), 0)
         nc.vector.memset(keys_plane[:].bitcast(I32), 0)
         warm_in = sb.tile([P, 1], F32)
         nc.vector.memset(warm_in[:], 0.0)
-        nc.vector.memset(f1[:], 0.0)
 
         def load_rows(queue, plane, scales, quad):
             queue.dma_start(
@@ -104,6 +103,9 @@ def tile_attend_gateway_madeside_kernel(tc, states, wq_words, wq_scales, keys_wo
             wq_codes.append(codes)
             wq_planes.append(plane)
 
+        f1 = sb.tile([P, T], F32, align_bytes=64, tag="wq_plane_then_f1")
+        nc.vector.memset(f1[:], 0.0)
+
         qv_ps = ps.tile([P, PACK, Q], F32)
         for t in range(PACK):
             nc.tensor.matmul_mx(out=qv_ps[:, t, :], lhsT=wq_codes[t // 2][:, t % 2, :].bitcast(FP8X4), lhsT_scale=wq_planes[t // 2][:, t % 2, :],
@@ -121,7 +123,7 @@ def tile_attend_gateway_madeside_kernel(tc, states, wq_words, wq_scales, keys_wo
             b_ps = ps.tile([P, last - first], F32, name="b_ps%d" % first)
             nc.tensor.matmul_mx(out=b_ps[:], lhsT=states_codes[:].bitcast(FP8X4), lhsT_scale=states_plane[:],
                                 rhs=notes_codes[:, cols].bitcast(FP8X4), rhs_scale=notes_plane[:, cols], start=True, stop=True)
-            if first == 0:
+            if last < U:
                 nc.scalar.copy(out=b_sb[:, cols], in_=b_ps[:])
             else:
                 nc.vector.tensor_copy(out=b_sb[:, cols], in_=b_ps[:])
@@ -135,14 +137,19 @@ def tile_attend_gateway_madeside_kernel(tc, states, wq_words, wq_scales, keys_wo
                                 start=True, stop=True)
             nc.vector.tensor_copy(out=a_sb[:, cols], in_=a_ps[:])
 
+        e2 = sb.tile([P, I], F32)
         for h in range(2):
-            lc = slice(LCOLS * h, LCOLS * (h + 1))
-            e2 = sb.tile([P, HALF], F32, name="e2_%d" % h)
-            nc.scalar.activation(out=e2[:], in_=b_sb[:].indirect(list2[:, lc]), func=ACT.Sigmoid,
-                                 bias=thr_col[:], scale=slope_col[:])
-            picked = sb.tile([P, HALF], F32, name="picked_%d" % h)
-            nc.scalar.activation(out=picked[:], in_=a_sb[:].indirect(list1[:, lc]), func=ACT.Copy)
-            nc.vector.tensor_tensor(out=f1[:].indirect(list1[:, lc]), in0=picked[:], in1=e2[:], op=ALU.mult)
+            nc.scalar.activation(out=e2[:, HALF * h : HALF * (h + 1)], in_=b_sb[:].indirect(list2[:, LCOLS * h : LCOLS * (h + 1)]),
+                                 func=ACT.Sigmoid, bias=thr_col[:], scale=slope_col[:])
+
+        head = list1[:, 0 : HEAD // 16]
+        rest = list1[:, HEAD // 16 : I // 16]
+        w_head = sb.tile([P, HEAD], F32)
+        nc.vector.tensor_tensor(out=w_head[:], in0=a_sb[:].indirect(head), in1=e2[:, 0:HEAD], op=ALU.mult)
+        nc.vector.tensor_copy(out=f1[:].indirect(head), in_=w_head[:])
+        a_rest = sb.tile([P, I - HEAD], F32)
+        nc.scalar.activation(out=a_rest[:], in_=a_sb[:].indirect(rest), func=ACT.Copy)
+        nc.vector.tensor_tensor(out=f1[:].indirect(rest), in0=a_rest[:], in1=e2[:, HEAD:I], op=ALU.mult)
 
         tt = sb.tile([P, T], F32)
         nc.vector.tensor_tensor(out=tt[:], in0=f1[:], in1=old_sb[:], op=ALU.add)

from contextlib import ExitStack

import concourse.mybir as mybir

D, K, T, U, I, Q = 512, 512, 1024, 1024, 512, 128
FLOPS = 2 * D * K * Q + 2 * K * Q * T + 2 * D * Q * U

F32 = mybir.dt.float32
BF16 = mybir.dt.bfloat16
I32 = mybir.dt.int32
U32 = mybir.dt.uint32
U16 = mybir.dt.uint16
U8 = mybir.dt.uint8
FP8X4 = mybir.dt.float8_e4m3fn_x4
FP4X4 = mybir.dt.float4_e2m1fn_x4
ACT = mybir.ActivationFunctionType
ALU = mybir.AluOpType

P = 128
PACK = 4
HALF = I // 2
LCOLS = HALF // 16
HEAD = 128


def tile_attend_gateway_madeside_kernel(tc, states, wq_words, wq_scales, keys_words, keys_scales,
                                         notes_words, notes_scales, thr, slope, old, offs, offs2, offs3, out):
    nc = tc.nc
    with ExitStack() as ctx:
        sb = ctx.enter_context(tc.tile_pool(name="sb", bufs=1))
        ps = ctx.enter_context(tc.psum_pool(name="ps", bufs=1))

        wq_plane_raw = sb.tile([P, K], U8, align_bytes=64, tag="wq_plane_then_f1")
        notes_plane = sb.tile([P, U], U8, align_bytes=64)
        keys_plane = sb.tile([P, T], U8, align_bytes=64)
        nc.vector.memset(wq_plane_raw[:].bitcast(I32), 0)
        nc.vector.memset(notes_plane[:].bitcast(I32), 0)
        nc.vector.memset(keys_plane[:].bitcast(I32), 0)
        warm_in = sb.tile([P, 1], F32)
        nc.vector.memset(warm_in[:], 0.0)

        def load_rows(queue, plane, scales, quad):
            queue.dma_start(
                out=plane[32 * quad : 32 * quad + 4, :].bitcast(I32),
                in_=scales[0, 4 * quad : 4 * quad + 4, :].bitcast(I32),
            )

        states_raw = sb.tile([P, PACK, Q], F32)
        wq_raw = sb.tile([P, K], U32)
        notes_codes = sb.tile([P, U], U32, align_bytes=64)
        keys_codes = sb.tile([P, 2 * T], U8, align_bytes=64)
        list1 = sb.tile([P, I // 16], U16)
        list2 = sb.tile([P, I // 16], U16)
        list3 = sb.tile([P, I // 16], U16)
        slope_col = sb.tile([P, 1], F32)
        thr_col = sb.tile([P, 1], F32)
        old_sb = sb.tile([P, T], F32)

        nc.sync.dma_start(out=states_raw[:], in_=states.rearrange("(p j) q -> p j q", j=PACK))
        for quad in (0, 1):
            load_rows(nc.sync, wq_plane_raw, wq_scales, quad)
        nc.sync.dma_start(out=wq_raw[:].bitcast(I32), in_=wq_words[0].rearrange("p n t -> p (n t)").bitcast(I32))
        load_rows(nc.sync, notes_plane, notes_scales, 0)
        nc.sync.dma_start(out=notes_codes[:].bitcast(I32), in_=notes_words[0].rearrange("p n t -> p (n t)").bitcast(I32))
        for quad in (1, 2):
            load_rows(nc.sync, notes_plane, notes_scales, quad)
        nc.sync.dma_start(out=keys_codes[:].bitcast(I32), in_=keys_words[0].bitcast(I32))
        for quad in range(3):
            load_rows(nc.sync, keys_plane, keys_scales, quad)
        nc.sync.dma_start(list2[:], offs2)
        nc.sync.dma_start(out=slope_col[:], in_=slope)
        nc.sync.dma_start(out=thr_col[:], in_=thr)
        nc.sync.dma_start(list1[:], offs)
        nc.sync.dma_start(list3[:], offs3)
        nc.sync.dma_start(out=old_sb[:], in_=old)

        for quad in (2, 3):
            load_rows(nc.scalar, wq_plane_raw, wq_scales, quad)

        load_rows(nc.gpsimd, notes_plane, notes_scales, 3)
        load_rows(nc.gpsimd, keys_plane, keys_scales, 3)

        warm_out = sb.tile([P, 1], F32)
        nc.scalar.activation(out=warm_out[:], in_=warm_in[:], func=ACT.Sigmoid)

        states_bf = sb.tile([P, Q, PACK], BF16, align_bytes=64)
        nc.vector.tensor_copy(out=states_bf[:], in_=states_raw[:].rearrange("p j q -> p q j"))
        states_codes = sb.tile([P, Q], U32, align_bytes=64)
        states_plane = sb.tile([P, Q], U8, align_bytes=64)
        nc.vector.quantize_mx(out=states_codes[:].bitcast(FP8X4), scales=states_plane[:],
                              in_=states_bf[:].rearrange("p q j -> p (q j)"))

        words_by_place = wq_raw[:].rearrange("p (m t) -> p m t", t=PACK)
        bytes_by_place = wq_plane_raw[:].rearrange("p (m t) -> p m t", t=PACK)
        wq_codes = []
        wq_planes = []
        for pair in range(2):
            places = slice(2 * pair, 2 * pair + 2)
            codes = sb.tile([P, 2, P], U32, align_bytes=64, name="wq_codes%d" % pair)
            nc.scalar.copy(out=codes[:].rearrange("p t m -> p m t"), in_=words_by_place[:, :, places])
            plane = sb.tile([P, 2, P], U8, align_bytes=64, name="wq_plane%d" % pair)
            nc.vector.tensor_copy(out=plane[:].rearrange("p t m -> p m t"), in_=bytes_by_place[:, :, places])
            wq_codes.append(codes)
            wq_planes.append(plane)

        f1 = sb.tile([P, T], F32, align_bytes=64, tag="wq_plane_then_f1")
        nc.vector.memset(f1[:], 0.0)

        qv_ps = ps.tile([P, PACK, Q], F32)
        for t in range(PACK):
            nc.tensor.matmul_mx(out=qv_ps[:, t, :], lhsT=wq_codes[t // 2][:, t % 2, :].bitcast(FP8X4), lhsT_scale=wq_planes[t // 2][:, t % 2, :],
                                rhs=states_codes[:].bitcast(FP8X4), rhs_scale=states_plane[:], start=True, stop=True)
        qv_bf = sb.tile([P, Q, PACK], BF16, align_bytes=64)
        nc.scalar.copy(out=qv_bf[:], in_=qv_ps[:].rearrange("p t q -> p q t"))
        qv_codes = sb.tile([P, Q], U32, align_bytes=64)
        qv_plane = sb.tile([P, Q], U8, align_bytes=64)
        nc.vector.quantize_mx(out=qv_codes[:].bitcast(FP8X4), scales=qv_plane[:],
                              in_=qv_bf[:].rearrange("p q j -> p (q j)"))

        b_sb = sb.tile([P, U], F32)
        for first, last in ((0, 512), (512, 768), (768, 1024)):
            cols = slice(first, last)
            b_ps = ps.tile([P, last - first], F32, name="b_ps%d" % first)
            nc.tensor.matmul_mx(out=b_ps[:], lhsT=states_codes[:].bitcast(FP8X4), lhsT_scale=states_plane[:],
                                rhs=notes_codes[:, cols].bitcast(FP8X4), rhs_scale=notes_plane[:, cols], start=True, stop=True)
            if last < U:
                nc.scalar.copy(out=b_sb[:, cols], in_=b_ps[:])
            else:
                nc.vector.tensor_copy(out=b_sb[:, cols], in_=b_ps[:])

        a_sb = sb.tile([P, T], F32)
        for c in range(4):
            cols = slice(256 * c, 256 * (c + 1))
            a_ps = ps.tile([P, 256], F32, name="a_ps%d" % c)
            nc.tensor.matmul_mx(out=a_ps[:], lhsT=qv_codes[:].bitcast(FP8X4), lhsT_scale=qv_plane[:],
                                rhs=keys_codes[:, 512 * c : 512 * (c + 1)].bitcast(FP4X4), rhs_scale=keys_plane[:, cols],
                                start=True, stop=True)
            nc.vector.tensor_copy(out=a_sb[:, cols], in_=a_ps[:])

        e2 = sb.tile([P, I], F32)
        for h in range(2):
            nc.scalar.activation(out=e2[:, HALF * h : HALF * (h + 1)], in_=b_sb[:].indirect(list2[:, LCOLS * h : LCOLS * (h + 1)]),
                                 func=ACT.Sigmoid, bias=thr_col[:], scale=slope_col[:])

        head = list1[:, 0 : HEAD // 16]
        rest = list1[:, HEAD // 16 : I // 16]
        w_head = sb.tile([P, HEAD], F32)
        nc.vector.tensor_tensor(out=w_head[:], in0=a_sb[:].indirect(head), in1=e2[:, 0:HEAD], op=ALU.mult)
        nc.vector.tensor_copy(out=f1[:].indirect(head), in_=w_head[:])
        a_rest = sb.tile([P, I - HEAD], F32)
        nc.scalar.activation(out=a_rest[:], in_=a_sb[:].indirect(rest), func=ACT.Copy)
        nc.vector.tensor_tensor(out=f1[:].indirect(rest), in0=a_rest[:], in1=e2[:, HEAD:I], op=ALU.mult)

        tt = sb.tile([P, T], F32)
        nc.vector.tensor_tensor(out=tt[:], in0=f1[:], in1=old_sb[:], op=ALU.add)

        y0 = sb.tile([P, HALF], F32)
        nc.scalar.activation(out=y0[:], in_=tt[:].indirect(list3[:, 0:LCOLS]), func=ACT.Copy)
        nc.scalar.dma_start(out=out[:, 0:HALF], in_=y0[:])
        y1 = sb.tile([P, HALF], F32)
        nc.vector.tensor_copy(out=y1[:], in_=tt[:].indirect(list3[:, LCOLS : 2 * LCOLS]))
        nc.sync.dma_start(out=out[:, HALF:I], in_=y1[:])
